import numpy as np
import ml_dtypes


def mxq(x, axis, fmt="e4m3"):
    dtype, down = {"e4m3": (ml_dtypes.float8_e4m3fn, 7), "e5m2": (ml_dtypes.float8_e5m2, 14)}[fmt]
    v = np.moveaxis(np.asarray(x, np.float32).astype(ml_dtypes.bfloat16).astype(np.float64), axis, -1)
    blocks = v.reshape(v.shape[:-1] + (-1, 32))
    amax = np.abs(blocks).max(-1, keepdims=True)
    byte = np.maximum(np.where(amax > 0, np.frexp(amax)[1] - 1 + 127, 0) - down, 1)
    scale = np.exp2(byte - 127.0)
    codes = (blocks / scale).astype(np.float32).astype(dtype).astype(np.float64)
    return np.moveaxis((codes * scale).reshape(v.shape), -1, axis)


WIDE = False


def mx_kscale(k):
    if not WIDE:
        return np.ones(k)
    levels = np.array([10, -10, 5, -5, 0])
    if k % 512:
        return np.exp2(np.random.permutation(np.resize(levels, k // 32))).repeat(32)
    a = np.empty((k // 512, 16))
    for p in range(k // 512):
        a[p, :8] = np.random.permutation(np.resize(levels, 8))
        for g in range(8):
            far = levels[np.abs(levels - a[p, g]) >= 10]
            a[p, g + 8] = far[np.random.randint(len(far))]
    return np.exp2(a.ravel()).repeat(32)


def f64(x):
    return np.asarray(x).astype(np.float64)


def striped(idx):
    return np.tile(idx.reshape(-1, 16).T, (8, 1)).astype(np.uint16)


def unstriped(offs):
    return offs[:16].T.reshape(-1).astype(np.int64)


def striped8(idx):
    return np.concatenate([x.reshape(-1, 16).T for x in idx]).astype(np.uint16)


def runs(offs, k):
    lists = np.stack([offs[16 * r : 16 * r + 16].T.reshape(-1) for r in range(8)]).astype(np.int64)
    return lists[np.arange(k) % 512 // 64]


def pack_weight(w):
    k, n = w.shape
    w = f64(np.asarray(w, np.float32).astype(ml_dtypes.bfloat16)).reshape(k // 32, 32, n)
    amax = np.abs(w).max(1)
    byte = np.clip(np.where(amax > 0, np.frexp(amax)[1] - 1 + 127 - 7, 1), 1, 254)
    scaled = (w * np.exp2(127.0 - byte)[:, None, :]).reshape(k, n).astype(np.float32)
    words = np.ascontiguousarray(scaled.reshape(k // 512, 128, 4, n).transpose(0, 1, 3, 2)).astype(ml_dtypes.float8_e4m3fn).view(np.uint8)
    return words, np.ascontiguousarray(byte.astype(np.uint8).reshape(k // 512, 16, n))


def unpack_weight(words, scales):
    g, p, n, _ = words.shape
    vals = np.ascontiguousarray(words).view(ml_dtypes.float8_e4m3fn).astype(np.float64) * np.repeat(np.exp2(scales.astype(np.float64) - 127.0), 8, axis=1)[..., None]
    return vals.transpose(0, 1, 3, 2).reshape(g * 512, n)


K, T, S, N, H = 512, 2048, 512, 512, 512


def setup_inputs():
    n = np.random.standard_normal
    s = mx_kscale(K)[:, None]
    u = mx_kscale(H)
    packed_xT = pack_weight(n((K, T)) * s)
    return {
        "x_words": packed_xT[0],
        "x_scales": packed_xT[1],
        "w1": (n((K, H)) / np.sqrt(K) / s).astype(np.float32),
        "gn": (np.random.uniform(0.5, 1.5, (H, 1)) * u[:, None]).astype(np.float32),
        "w2": (n((H, N)) / np.sqrt(H) / u[:, None]).astype(np.float32),
        "offs": striped(np.random.permutation(T)[:S]),
        "n1": striped8(np.stack([np.random.permutation(S) for _ in range(8)])),
        "n2": striped8(np.stack([np.random.permutation(S) for _ in range(8)])),
        "n3": striped8(np.stack([np.random.permutation(S) for _ in range(8)])),
        "n4": striped8(np.stack([np.random.permutation(S) for _ in range(8)])),
        "n5": striped8(np.stack([np.random.permutation(S) for _ in range(8)])),
    }


def reference(x_words, x_scales, w1, gn, w2, offs, n1, n2, n3, n4, n5):
    xq = unpack_weight(x_words, x_scales)[:, unstriped(offs)]
    y = mxq(f64(w1), 0, "e4m3").T @ xq
    z = f64(gn) * (np.maximum(y, y[np.arange(H)[:, None], runs(n1, H)]) - (np.maximum(y[np.arange(H)[:, None], runs(n2, H)], y[np.arange(H)[:, None], runs(n3, H)])))
    h = mxq(f64(w2), 0, "e4m3").T @ mxq(z, 0, "e4m3")
    return np.maximum(h, y[np.arange(H)[:, None], runs(n5, H)]) - (np.minimum(h[np.arange(N)[:, None], runs(n4, N)], y))

@@ -1,0 +1,161 @@
+from contextlib import ExitStack
+
+import concourse.mybir as mybir
+
+K, T, S, N, H = 512, 2048, 512, 512, 512
+FLOPS = 2 * K * H * S + 2 * H * N * S
+
+F32 = mybir.dt.float32
+BF16 = mybir.dt.bfloat16
+I32 = mybir.dt.int32
+U32 = mybir.dt.uint32
+U16 = mybir.dt.uint16
+U8 = mybir.dt.uint8
+FP8X4 = mybir.dt.float8_e4m3fn_x4
+ALU = mybir.AluOpType
+ACT = mybir.ActivationFunctionType
+
+P = 128
+PACK = 4
+WINDOW = 2 * S
+
+
+def tile_picked_skipmaxbmix_none_p_kernel(tc, x_words, x_scales, w1, gn, w2, offs, n1, n2, n3, n4, n5, out):
+    nc = tc.nc
+    with ExitStack() as ctx:
+        keep = ctx.enter_context(tc.tile_pool(name="keep", bufs=1))
+        psum = ctx.enter_context(tc.psum_pool(name="psum", bufs=1))
+
+        def f32_tile(name):
+            return keep.tile([P, S], F32, name=name)
+
+        def load_list(src, name):
+            tile = keep.tile([P, S // 16], U16, name=name)
+            nc.sync.dma_start(tile[:], src)
+            return tile
+
+        xs_all = keep.tile([P, T], U8, name="xs_all")
+        nc.vector.memset(xs_all[:].bitcast(I32), 0)
+        offs_sb = load_list(offs, "offs_sb")
+        for q in range(4):
+            nc.sync.dma_start(xs_all[32 * q : 32 * q + 4, :].bitcast(I32), x_scales[0, 4 * q : 4 * q + 4, :].bitcast(I32))
+        w1_raw = keep.tile([P, PACK, H], F32, name="w1_raw")
+        nc.sync.dma_start(w1_raw[:], w1.rearrange("(p j) c -> p j c", j=PACK))
+        xw_all = keep.tile([P, T], I32, name="xw_all")
+        nc.sync.dma_start(xw_all[:], x_words[0].rearrange("p n t -> p (n t)").bitcast(I32))
+        n2_sb = load_list(n2, "n2_sb")
+        n3_sb = load_list(n3, "n3_sb")
+        n1_sb = load_list(n1, "n1_sb")
+        w2_raw = keep.tile([P, PACK, N], F32, name="w2_raw")
+        nc.sync.dma_start(w2_raw[:], w2.rearrange("(p j) c -> p j c", j=PACK))
+        gn_sb = keep.tile([P, PACK], F32, name="gn_sb")
+        nc.sync.dma_start(gn_sb[:], gn.rearrange("(p t) o -> p (t o)", t=PACK))
+        n5_sb = load_list(n5, "n5_sb")
+        n4_sb = load_list(n4, "n4_sb")
+
+        xs = keep.tile([P, S], U8, name="xs", align_bytes=64)
+        nc.vector.tensor_copy(xs[:], xs_all[:].indirect(offs_sb[:]))
+        w1_bf = keep.tile([P, PACK * H], BF16, name="w1_bf", align_bytes=64)
+        nc.vector.tensor_copy(
+            w1_bf[:].rearrange("p (t m j) -> p m j t", t=PACK, j=PACK),
+            w1_raw[:].rearrange("p j (m t) -> p m j t", t=PACK),
+        )
+        w1_codes = keep.tile([P, H], U32, name="w1_codes", align_bytes=64)
+        w1_scales = keep.tile([P, H], U8, name="w1_scales", align_bytes=64)
+        nc.vector.quantize_mx(out=w1_codes[:].bitcast(FP8X4), scales=w1_scales[:], in_=w1_bf[:])
+        xw = keep.tile([P, S], U32, name="xw", tag="xw_then_w2", align_bytes=64)
+        nc.vector.tensor_copy(xw[:], xw_all[:].bitcast(U32).indirect(offs_sb[:]))
+
+        y_ps, y_win = [], []
+        for t in range(PACK):
+            cols = slice(P * t, P * (t + 1))
+            bank = psum.tile([P, S], F32, name=f"y_ps{t}")
+            nc.tensor.matmul_mx(out=bank[:], lhsT=w1_codes[:, cols].bitcast(FP8X4), lhsT_scale=w1_scales[:, cols],
+                                rhs=xw[:].bitcast(FP8X4), rhs_scale=xs[:], start=True, stop=True)
+            win = keep.tile([P, WINDOW], F32, name=f"y_win{t}")
+            nc.scalar.copy(win[:, :S], bank[:])
+            y_ps.append(bank)
+            y_win.append(win)
+
+        z_bf = keep.tile([P, S, PACK], BF16, name="z_bf", tag="z_then_g5", align_bytes=64)
+        max23 = {}
+
+        def larger_of_n2_n3(t):
+            g2, g3, excess, larger = (f32_tile(f"{name}{t}") for name in ("g2_", "g3_", "excess", "max23_"))
+            diff = max23[t - 1][1] if t else f32_tile("diff0")
+            nc.vector.tensor_copy(g2[:], y_win[t][:].indirect(n2_sb[:]))
+            nc.vector.tensor_copy(g3[:], y_win[t][:].indirect(n3_sb[:]))
+            nc.gpsimd.tensor_tensor(diff[:], g3[:], g2[:], ALU.subtract)
+            nc.scalar.activation(excess[:], diff[:], ACT.Relu)
+            max23[t] = (g2, excess, larger)
+
+        def finish_max23(t):
+            g2, excess, larger = max23[t]
+            nc.gpsimd.tensor_tensor(larger[:], g2[:], excess[:], ALU.add)
+
+        def z_tile(t):
+            g1, max01, zraw = (f32_tile(f"{name}{t}") for name in ("g1_", "max01_", "zraw"))
+            g1_tiles.append(g1)
+            nc.vector.tensor_copy(g1[:], y_win[t][:].indirect(n1_sb[:]))
+            nc.vector.tensor_tensor(max01[:], y_ps[t][:], g1[:], ALU.max)
+            nc.gpsimd.tensor_tensor(zraw[:], max01[:], max23[t][2][:], ALU.subtract)
+            nc.scalar.activation(z_bf[:, :, t], zraw[:], ACT.Copy, scale=gn_sb[:, t : t + 1])
+
+        larger_of_n2_n3(0)
+        finish_max23(0)
+        g1_tiles = []
+        for t in range(PACK):
+            if t + 1 < PACK:
+                larger_of_n2_n3(t + 1)
+            z_tile(t)
+            if t + 1 < PACK:
+                finish_max23(t + 1)
+
+        w2_bf = keep.tile([P, PACK * N], BF16, name="w2_bf", tag="xw_then_w2", align_bytes=64)
+        for piece in range(4):
+            ms = slice(32 * piece, 32 * (piece + 1))
+            nc.scalar.copy(
+                w2_bf[:].rearrange("p (t m j) -> p m j t", t=PACK, j=PACK)[:, ms],
+                w2_raw[:].rearrange("p j (m t) -> p m j t", t=PACK)[:, ms],
+            )
+
+        w2_codes = keep.tile([P, N], U32, name="w2_codes", align_bytes=64)
+        w2_scales = keep.tile([P, N], U8, name="w2_scales", align_bytes=64)
+        nc.vector.quantize_mx(out=w2_codes[:].bitcast(FP8X4), scales=w2_scales[:], in_=w2_bf[:])
+        g5 = [g1_tiles[PACK - 1][:], y_win[0][:, S:], y_win[1][:, S:]]
+        for t in range(PACK - 1):
+            nc.vector.tensor_copy(g5[t], y_win[t][:].indirect(n5_sb[:]))
+        z_codes = keep.tile([P, S], U32, name="z_codes", align_bytes=64)
+        z_scales = keep.tile([P, S], U8, name="z_scales", align_bytes=64)
+        nc.vector.quantize_mx(out=z_codes[:].bitcast(FP8X4), scales=z_scales[:], in_=z_bf[:].rearrange("p s t -> p (s t)"))
+        g5_last = keep.tile([P, S], F32, name="g5_last", tag="z_then_g5", align_bytes=64)
+        g5.append(g5_last[:])
+        nc.vector.tensor_copy(g5[PACK - 1], y_win[PACK - 1][:].indirect(n5_sb[:]))
+
+        h_ps = []
+        for t in range(PACK):
+            cols = slice(P * t, P * (t + 1))
+            bank = psum.tile([P, S], F32, name=f"h_ps{t}")
+            nc.tensor.matmul_mx(out=bank[:], lhsT=w2_codes[:, cols].bitcast(FP8X4), lhsT_scale=w2_scales[:, cols],
+                                rhs=z_codes[:].bitcast(FP8X4), rhs_scale=z_scales[:], start=True, stop=True)
+            h_ps.append(bank)
+        h_win = [keep.tile([P, WINDOW], F32, name=f"h_win{t}") for t in range(PACK)]
+        upper = [f32_tile(f"upper{t}") for t in range(PACK)]
+        out_rows = out.rearrange("(p t) s -> p t s", t=PACK)
+
+        def larger_of_h_n5(t):
+            nc.vector.tensor_tensor(upper[t][:], h_ps[t][:], g5[t], ALU.max)
+
+        nc.scalar.copy(h_win[0][:, :S], h_ps[0][:])
+        larger_of_h_n5(1)
+        for t in range(1, PACK):
+            nc.scalar.copy(h_win[t][:, :S], h_ps[t][:])
+        for t in range(PACK):
+            g4, lower, res = (f32_tile(f"{name}{t}") for name in ("g4_", "lower", "res"))
+            nc.vector.tensor_copy(g4[:], h_win[t][:].indirect(n4_sb[:]))
+            if t != 1:
+                larger_of_h_n5(t)
+            nc.vector.tensor_tensor(lower[:], y_ps[t][:], g4[:], ALU.min)
+            engine = nc.gpsimd if t + 1 < PACK else nc.vector
+            engine.tensor_tensor(res[:], upper[t][:], lower[:], ALU.subtract)
+            nc.sync.dma_start(out_rows[:, t, :], res[:])

@@ -17,7 +17,10 @@ ACT = mybir.ActivationFunctionType
 
 P = 128
 PACK = 4
+LAST = PACK - 1
 WINDOW = 2 * S
+HALF = S // 2
+HALVES = (slice(0, HALF), slice(HALF, S))
 
 
 def tile_picked_skipmaxbmix_none_p_kernel(tc, x_words, x_scales, w1, gn, w2, offs, n1, n2, n3, n4, n5, out):
@@ -34,13 +37,20 @@ def tile_picked_skipmaxbmix_none_p_kernel(tc, x_words, x_scales, w1, gn, w2, off
             nc.sync.dma_start(tile[:], src)
             return tile
 
+        def quantize(values, name, tag=None):
+            width = values.shape[1] // PACK
+            codes = keep.tile([P, width], U32, name=f"{name}_codes", tag=tag or f"{name}_codes", align_bytes=64)
+            scales = keep.tile([P, width], U8, name=f"{name}_scales", align_bytes=64)
+            nc.vector.quantize_mx(out=codes[:].bitcast(FP8X4), scales=scales[:], in_=values)
+            return codes, scales
+
         xs_all = keep.tile([P, T], U8, name="xs_all")
         nc.vector.memset(xs_all[:].bitcast(I32), 0)
-        offs_sb = load_list(offs, "offs_sb")
-        for q in range(4):
-            nc.sync.dma_start(xs_all[32 * q : 32 * q + 4, :].bitcast(I32), x_scales[0, 4 * q : 4 * q + 4, :].bitcast(I32))
         w1_raw = keep.tile([P, PACK, H], F32, name="w1_raw")
         nc.sync.dma_start(w1_raw[:], w1.rearrange("(p j) c -> p j c", j=PACK))
+        for q in range(4):
+            nc.sync.dma_start(xs_all[32 * q : 32 * q + 4, :].bitcast(I32), x_scales[0, 4 * q : 4 * q + 4, :].bitcast(I32))
+        offs_sb = load_list(offs, "offs_sb")
         xw_all = keep.tile([P, T], I32, name="xw_all")
         nc.sync.dma_start(xw_all[:], x_words[0].rearrange("p n t -> p (n t)").bitcast(I32))
         n2_sb = load_list(n2, "n2_sb")
@@ -53,62 +63,72 @@ def tile_picked_skipmaxbmix_none_p_kernel(tc, x_words, x_scales, w1, gn, w2, off
         n5_sb = load_list(n5, "n5_sb")
         n4_sb = load_list(n4, "n4_sb")
 
+        w1_view = w1_raw[:].rearrange("p j (m t) -> p m j t", t=PACK)
+        w1_bf = [keep.tile([P, 2 * PACK * P], BF16, name=f"w1_bf{u}", align_bytes=64) for u in range(2)]
+        w1_out = [tile[:].rearrange("p (t m j) -> p m j t", t=2, j=PACK) for tile in w1_bf]
+        nc.vector.tensor_copy(w1_out[0], w1_view[:, :, :, 0:2])
+        nc.scalar.copy(w1_out[1], w1_view[:, :, :, 2:4])
         xs = keep.tile([P, S], U8, name="xs", align_bytes=64)
         nc.vector.tensor_copy(xs[:], xs_all[:].indirect(offs_sb[:]))
-        w1_bf = keep.tile([P, PACK * H], BF16, name="w1_bf", align_bytes=64)
-        nc.vector.tensor_copy(
-            w1_bf[:].rearrange("p (t m j) -> p m j t", t=PACK, j=PACK),
-            w1_raw[:].rearrange("p j (m t) -> p m j t", t=PACK),
-        )
-        w1_codes = keep.tile([P, H], U32, name="w1_codes", align_bytes=64)
-        w1_scales = keep.tile([P, H], U8, name="w1_scales", align_bytes=64)
-        nc.vector.quantize_mx(out=w1_codes[:].bitcast(FP8X4), scales=w1_scales[:], in_=w1_bf[:])
+        w1_q = [quantize(w1_bf[0][:], "w1a")]
         xw = keep.tile([P, S], U32, name="xw", tag="xw_then_w2", align_bytes=64)
-        nc.vector.tensor_copy(xw[:], xw_all[:].bitcast(U32).indirect(offs_sb[:]))
+        for u, cols in enumerate(HALVES):
+            nc.vector.tensor_copy(xw[:, cols], xw_all[:].bitcast(U32).indirect(offs_sb[:, 16 * u : 16 * (u + 1)]))
+        w1_q.append(quantize(w1_bf[1][:], "w1b"))
 
-        y_ps, y_win = [], []
-        for t in range(PACK):
-            cols = slice(P * t, P * (t + 1))
-            bank = psum.tile([P, S], F32, name=f"y_ps{t}")
-            nc.tensor.matmul_mx(out=bank[:], lhsT=w1_codes[:, cols].bitcast(FP8X4), lhsT_scale=w1_scales[:, cols],
-                                rhs=xw[:].bitcast(FP8X4), rhs_scale=xs[:], start=True, stop=True)
-            win = keep.tile([P, WINDOW], F32, name=f"y_win{t}")
-            nc.scalar.copy(win[:, :S], bank[:])
-            y_ps.append(bank)
-            y_win.append(win)
+        def y_product(bank, t, cols):
+            codes, scales = w1_q[t // 2]
+            rows = slice(P * (t % 2), P * (t % 2 + 1))
+            nc.tensor.matmul_mx(out=bank[:, cols], lhsT=codes[:, rows].bitcast(FP8X4), lhsT_scale=scales[:, rows],
+                                rhs=xw[:, cols].bitcast(FP8X4), rhs_scale=xs[:, cols], start=True, stop=True)
 
-        z_bf = keep.tile([P, S, PACK], BF16, name="z_bf", tag="z_then_g5", align_bytes=64)
-        max23 = {}
+        y_ps = [psum.tile([P, S], F32, name=f"y_ps{t}") for t in range(PACK)]
+        h_ps = [psum.tile([P, S], F32, name=f"h_ps{t}") for t in range(PACK)]
+        y_win = [keep.tile([P, WINDOW], F32, name=f"y_win{t}", tag=f"y_win{t}", align_bytes=64) for t in range(PACK)]
+        for bank, cols in zip((h_ps[LAST], y_ps[0]), HALVES):
+            y_product(bank, 0, cols)
+            nc.scalar.copy(y_win[0][:, cols], bank[:, cols])
+        for t in range(1, PACK):
+            y_product(y_ps[t], t, slice(0, S))
+            nc.scalar.copy(y_win[t][:, :S], y_ps[t][:])
+        y_product(y_ps[0], 0, HALVES[0])
 
-        def larger_of_n2_n3(t):
-            g2, g3, excess, larger = (f32_tile(f"{name}{t}") for name in ("g2_", "g3_", "excess", "max23_"))
-            diff = max23[t - 1][1] if t else f32_tile("diff0")
+        z_bf = [keep.tile([P, HALF, PACK], BF16, name="z_bf0", align_bytes=64),
+                keep.tile([P, HALF, PACK], BF16, name="z_bf1", tag="z_then_g5", align_bytes=64)]
+        g2_tiles, excess_tiles, max23_tiles, g1_tiles = [], [], [], []
+
+        def start_max23(t):
+            g2, g3, excess = (f32_tile(f"{name}{t}") for name in ("g2_", "g3_", "excess"))
+            diff = excess_tiles[t - 1] if t else f32_tile("diff0")
             nc.vector.tensor_copy(g2[:], y_win[t][:].indirect(n2_sb[:]))
             nc.vector.tensor_copy(g3[:], y_win[t][:].indirect(n3_sb[:]))
             nc.gpsimd.tensor_tensor(diff[:], g3[:], g2[:], ALU.subtract)
             nc.scalar.activation(excess[:], diff[:], ACT.Relu)
-            max23[t] = (g2, excess, larger)
+            g2_tiles.append(g2)
+            excess_tiles.append(excess)
 
         def finish_max23(t):
-            g2, excess, larger = max23[t]
-            nc.gpsimd.tensor_tensor(larger[:], g2[:], excess[:], ALU.add)
+            larger = f32_tile(f"max23_{t}")
+            nc.gpsimd.tensor_tensor(larger[:], g2_tiles[t][:], excess_tiles[t][:], ALU.add)
+            max23_tiles.append(larger)
 
         def z_tile(t):
             g1, max01, zraw = (f32_tile(f"{name}{t}") for name in ("g1_", "max01_", "zraw"))
             g1_tiles.append(g1)
             nc.vector.tensor_copy(g1[:], y_win[t][:].indirect(n1_sb[:]))
             nc.vector.tensor_tensor(max01[:], y_ps[t][:], g1[:], ALU.max)
-            nc.gpsimd.tensor_tensor(zraw[:], max01[:], max23[t][2][:], ALU.subtract)
-            nc.scalar.activation(z_bf[:, :, t], zraw[:], ACT.Copy, scale=gn_sb[:, t : t + 1])
+            for cols in HALVES if t == LAST else (slice(0, S),):
+                nc.gpsimd.tensor_tensor(zraw[:, cols], max01[:, cols], max23_tiles[t][:, cols], ALU.subtract)
+            for u, cols in enumerate(HALVES):
+                nc.scalar.activation(z_bf[u][:, :, t], zraw[:, cols], ACT.Copy, scale=gn_sb[:, t : t + 1])
 
-        larger_of_n2_n3(0)
+        start_max23(0)
         finish_max23(0)
-        g1_tiles = []
         for t in range(PACK):
-            if t + 1 < PACK:
-                larger_of_n2_n3(t + 1)
+            if t < LAST:
+                start_max23(t + 1)
             z_tile(t)
-            if t + 1 < PACK:
+            if t < LAST:
                 finish_max23(t + 1)
 
         w2_bf = keep.tile([P, PACK * N], BF16, name="w2_bf", tag="xw_then_w2", align_bytes=64)
@@ -118,44 +138,45 @@ def tile_picked_skipmaxbmix_none_p_kernel(tc, x_words, x_scales, w1, gn, w2, off
                 w2_bf[:].rearrange("p (t m j) -> p m j t", t=PACK, j=PACK)[:, ms],
                 w2_raw[:].rearrange("p j (m t) -> p m j t", t=PACK)[:, ms],
             )
-
-        w2_codes = keep.tile([P, N], U32, name="w2_codes", align_bytes=64)
-        w2_scales = keep.tile([P, N], U8, name="w2_scales", align_bytes=64)
-        nc.vector.quantize_mx(out=w2_codes[:].bitcast(FP8X4), scales=w2_scales[:], in_=w2_bf[:])
-        g5 = [g1_tiles[PACK - 1][:], y_win[0][:, S:], y_win[1][:, S:]]
-        for t in range(PACK - 1):
+        g5 = [g1_tiles[LAST][:], y_win[0][:, S:], y_win[1][:, S:]]
+        for t in range(LAST):
             nc.vector.tensor_copy(g5[t], y_win[t][:].indirect(n5_sb[:]))
-        z_codes = keep.tile([P, S], U32, name="z_codes", align_bytes=64)
-        z_scales = keep.tile([P, S], U8, name="z_scales", align_bytes=64)
-        nc.vector.quantize_mx(out=z_codes[:].bitcast(FP8X4), scales=z_scales[:], in_=z_bf[:].rearrange("p s t -> p (s t)"))
+        w2_codes, w2_scales = quantize(w2_bf[:], "w2", tag=f"y_win{LAST - 1}")
+        z_q = [quantize(z_bf[u][:].rearrange("p s t -> p (s t)"), f"z{u}") for u in range(2)]
         g5_last = keep.tile([P, S], F32, name="g5_last", tag="z_then_g5", align_bytes=64)
         g5.append(g5_last[:])
-        nc.vector.tensor_copy(g5[PACK - 1], y_win[PACK - 1][:].indirect(n5_sb[:]))
+        nc.vector.tensor_copy(g5[LAST], y_win[LAST][:].indirect(n5_sb[:]))
 
-        h_ps = []
-        for t in range(PACK):
-            cols = slice(P * t, P * (t + 1))
-            bank = psum.tile([P, S], F32, name=f"h_ps{t}")
-            nc.tensor.matmul_mx(out=bank[:], lhsT=w2_codes[:, cols].bitcast(FP8X4), lhsT_scale=w2_scales[:, cols],
-                                rhs=z_codes[:].bitcast(FP8X4), rhs_scale=z_scales[:], start=True, stop=True)
-            h_ps.append(bank)
+        for u, half in enumerate(HALVES):
+            for t in range(PACK):
+                cols = slice(P * t, P * (t + 1))
+                nc.tensor.matmul_mx(out=h_ps[t][:, half], lhsT=w2_codes[:, cols].bitcast(FP8X4), lhsT_scale=w2_scales[:, cols],
+                                    rhs=z_q[u][0][:].bitcast(FP8X4), rhs_scale=z_q[u][1][:], start=True, stop=True)
         h_win = [keep.tile([P, WINDOW], F32, name=f"h_win{t}") for t in range(PACK)]
         upper = [f32_tile(f"upper{t}") for t in range(PACK)]
         out_rows = out.rearrange("(p t) s -> p t s", t=PACK)
 
-        def larger_of_h_n5(t):
-            nc.vector.tensor_tensor(upper[t][:], h_ps[t][:], g5[t], ALU.max)
-
-        nc.scalar.copy(h_win[0][:, :S], h_ps[0][:])
-        larger_of_h_n5(1)
-        for t in range(1, PACK):
-            nc.scalar.copy(h_win[t][:, :S], h_ps[t][:])
         for t in range(PACK):
-            g4, lower, res = (f32_tile(f"{name}{t}") for name in ("g4_", "lower", "res"))
+            nc.scalar.copy(h_win[t][:, :S], h_ps[t][:])
+        diff5, excess5 = f32_tile("diff5"), f32_tile("excess5")
+        nc.gpsimd.tensor_tensor(diff5[:], g5[LAST], h_win[LAST][:, :S], ALU.subtract)
+        nc.scalar.activation(excess5[:], diff5[:], ACT.Relu)
+        res_tiles = (g5_last, excess5, f32_tile("res2"))
+        for t in range(LAST):
+            g4, lower = (f32_tile(f"{name}{t}") for name in ("g4_", "lower"))
+            res = res_tiles[t]
             nc.vector.tensor_copy(g4[:], h_win[t][:].indirect(n4_sb[:]))
-            if t != 1:
-                larger_of_h_n5(t)
+            nc.vector.tensor_tensor(upper[t][:], h_ps[t][:], g5[t], ALU.max)
             nc.vector.tensor_tensor(lower[:], y_ps[t][:], g4[:], ALU.min)
-            engine = nc.gpsimd if t + 1 < PACK else nc.vector
-            engine.tensor_tensor(res[:], upper[t][:], lower[:], ALU.subtract)
+            nc.gpsimd.tensor_tensor(res[:], upper[t][:], lower[:], ALU.subtract)
             nc.sync.dma_start(out_rows[:, t, :], res[:])
+            if t == 0:
+                nc.gpsimd.tensor_tensor(upper[LAST][:], h_win[LAST][:, :S], excess5[:], ALU.add)
+        g4, lower, res = (f32_tile(f"{name}{LAST}") for name in ("g4_", "lower", "res"))
+        for u, cols in enumerate(HALVES):
+            nc.vector.tensor_copy(g4[:, cols], h_win[LAST][:].indirect(n4_sb[:, 16 * u : 16 * (u + 1)]))
+        for cols in HALVES:
+            nc.vector.tensor_tensor(lower[:, cols], y_ps[LAST][:, cols], g4[:, cols], ALU.min)
+        for cols in HALVES:
+            nc.vector.tensor_tensor(res[:, cols], upper[LAST][:, cols], lower[:, cols], ALU.subtract)
+            nc.sync.dma_start(out_rows[:, LAST, cols], res[:, cols])

@@ -1,6 +1,7 @@
 from contextlib import ExitStack
 
 import concourse.mybir as mybir
+from concourse.masks import make_identity
 
 K, T, S, N, H = 512, 2048, 512, 512, 512
 FLOPS = 2 * K * H * S + 2 * H * N * S
@@ -44,6 +45,9 @@ def tile_picked_skipmaxbmix_none_p_kernel(tc, x_words, x_scales, w1, gn, w2, off
             nc.vector.quantize_mx(out=codes[:].bitcast(FP8X4), scales=scales[:], in_=values)
             return codes, scales
 
+        identity = keep.tile([P, P], F32, name="identity")
+        make_identity(nc, identity[:])
+
         xs_all = keep.tile([P, T], U8, name="xs_all")
         nc.vector.memset(xs_all[:].bitcast(I32), 0)
         w1_raw = keep.tile([P, PACK, H], F32, name="w1_raw")
@@ -51,7 +55,7 @@ def tile_picked_skipmaxbmix_none_p_kernel(tc, x_words, x_scales, w1, gn, w2, off
         for q in range(4):
             nc.sync.dma_start(xs_all[32 * q : 32 * q + 4, :].bitcast(I32), x_scales[0, 4 * q : 4 * q + 4, :].bitcast(I32))
         offs_sb = load_list(offs, "offs_sb")
-        xw_all = keep.tile([P, T], I32, name="xw_all")
+        xw_all = keep.tile([P, T], I32, name="xw_all", tag="xw_all", align_bytes=64)
         nc.sync.dma_start(xw_all[:], x_words[0].rearrange("p n t -> p (n t)").bitcast(I32))
         n2_sb = load_list(n2, "n2_sb")
         n3_sb = load_list(n3, "n3_sb")
@@ -74,7 +78,7 @@ def tile_picked_skipmaxbmix_none_p_kernel(tc, x_words, x_scales, w1, gn, w2, off
         xw = keep.tile([P, S], U32, name="xw", tag="xw_then_w2", align_bytes=64)
         for u, cols in enumerate(HALVES):
             nc.vector.tensor_copy(xw[:, cols], xw_all[:].bitcast(U32).indirect(offs_sb[:, 16 * u : 16 * (u + 1)]))
-        w1_q.append(quantize(w1_bf[1][:], "w1b"))
+        w1_q.append(quantize(w1_bf[1][:], "w1b", tag="xw_all"))
 
         def y_product(bank, t, cols):
             codes, scales = w1_q[t // 2]
@@ -102,14 +106,16 @@ def tile_picked_skipmaxbmix_none_p_kernel(tc, x_words, x_scales, w1, gn, w2, off
             diff = excess_tiles[t - 1] if t else f32_tile("diff0")
             nc.vector.tensor_copy(g2[:], y_win[t][:].indirect(n2_sb[:]))
             nc.vector.tensor_copy(g3[:], y_win[t][:].indirect(n3_sb[:]))
-            nc.gpsimd.tensor_tensor(diff[:], g3[:], g2[:], ALU.subtract)
-            nc.scalar.activation(excess[:], diff[:], ACT.Relu)
+            for cols in HALVES if t == 0 else (slice(0, S),):
+                nc.gpsimd.tensor_tensor(diff[:, cols], g3[:, cols], g2[:, cols], ALU.subtract)
+                nc.scalar.activation(excess[:, cols], diff[:, cols], ACT.Relu)
             g2_tiles.append(g2)
             excess_tiles.append(excess)
 
         def finish_max23(t):
             larger = f32_tile(f"max23_{t}")
-            nc.gpsimd.tensor_tensor(larger[:], g2_tiles[t][:], excess_tiles[t][:], ALU.add)
+            for cols in HALVES if t == 0 else (slice(0, S),):
+                nc.gpsimd.tensor_tensor(larger[:, cols], g2_tiles[t][:, cols], excess_tiles[t][:, cols], ALU.add)
             max23_tiles.append(larger)
 
         def z_tile(t):
@@ -138,45 +144,72 @@ def tile_picked_skipmaxbmix_none_p_kernel(tc, x_words, x_scales, w1, gn, w2, off
                 w2_bf[:].rearrange("p (t m j) -> p m j t", t=PACK, j=PACK)[:, ms],
                 w2_raw[:].rearrange("p j (m t) -> p m j t", t=PACK)[:, ms],
             )
-        g5 = [g1_tiles[LAST][:], y_win[0][:, S:], y_win[1][:, S:]]
+        g5 = [g1_tiles[LAST - 1][:], g1_tiles[LAST][:], y_win[0][:, S:]]
         for t in range(LAST):
             nc.vector.tensor_copy(g5[t], y_win[t][:].indirect(n5_sb[:]))
-        w2_codes, w2_scales = quantize(w2_bf[:], "w2", tag=f"y_win{LAST - 1}")
-        z_q = [quantize(z_bf[u][:].rearrange("p s t -> p (s t)"), f"z{u}") for u in range(2)]
+        w2_codes, w2_scales = quantize(w2_bf[:], "w2", tag="y_win1")
+        z_codes = keep.tile([P, S], U32, name="z_codes", align_bytes=64)
+        z_scales = keep.tile([P, S], U8, name="z_scales", align_bytes=64)
+        for u, half in enumerate(HALVES):
+            nc.vector.quantize_mx(out=z_codes[:, half].bitcast(FP8X4), scales=z_scales[:, half],
+                                  in_=z_bf[u][:].rearrange("p s t -> p (s t)"))
         g5_last = keep.tile([P, S], F32, name="g5_last", tag="z_then_g5", align_bytes=64)
         g5.append(g5_last[:])
         nc.vector.tensor_copy(g5[LAST], y_win[LAST][:].indirect(n5_sb[:]))
 
-        for u, half in enumerate(HALVES):
-            for t in range(PACK):
-                cols = slice(P * t, P * (t + 1))
-                nc.tensor.matmul_mx(out=h_ps[t][:, half], lhsT=w2_codes[:, cols].bitcast(FP8X4), lhsT_scale=w2_scales[:, cols],
-                                    rhs=z_q[u][0][:].bitcast(FP8X4), rhs_scale=z_q[u][1][:], start=True, stop=True)
-        h_win = [keep.tile([P, WINDOW], F32, name=f"h_win{t}") for t in range(PACK)]
-        upper = [f32_tile(f"upper{t}") for t in range(PACK)]
+        for t in range(PACK):
+            rows = slice(P * t, P * (t + 1))
+            for cols in HALVES if t == 0 else (slice(0, S),):
+                nc.tensor.matmul_mx(out=h_ps[t][:, cols], lhsT=w2_codes[:, rows].bitcast(FP8X4), lhsT_scale=w2_scales[:, rows],
+                                    rhs=z_codes[:, cols].bitcast(FP8X4), rhs_scale=z_scales[:, cols], start=True, stop=True)
+        neg_h_win = [keep.tile([P, WINDOW], F32, name=f"neg_h_win{t}") for t in range(PACK)]
         out_rows = out.rearrange("(p t) s -> p t s", t=PACK)
+        blocks = [slice(P * c, P * (c + 1)) for c in range(S // P)]
 
         for t in range(PACK):
-            nc.scalar.copy(h_win[t][:, :S], h_ps[t][:])
-        diff5, excess5 = f32_tile("diff5"), f32_tile("excess5")
-        nc.gpsimd.tensor_tensor(diff5[:], g5[LAST], h_win[LAST][:, :S], ALU.subtract)
-        nc.scalar.activation(excess5[:], diff5[:], ACT.Relu)
-        res_tiles = (g5_last, excess5, f32_tile("res2"))
-        for t in range(LAST):
-            g4, lower = (f32_tile(f"{name}{t}") for name in ("g4_", "lower"))
-            res = res_tiles[t]
-            nc.vector.tensor_copy(g4[:], h_win[t][:].indirect(n4_sb[:]))
-            nc.vector.tensor_tensor(upper[t][:], h_ps[t][:], g5[t], ALU.max)
-            nc.vector.tensor_tensor(lower[:], y_ps[t][:], g4[:], ALU.min)
-            nc.gpsimd.tensor_tensor(res[:], upper[t][:], lower[:], ALU.subtract)
+            nc.scalar.activation(neg_h_win[t][:, :S], h_ps[t][:], ACT.Copy, scale=-1.0)
+
+        def excess_of_h(t):
+            gap, over = f32_tile(f"gap{t}"), f32_tile(f"over{t}")
+            nc.gpsimd.tensor_tensor(gap[:], g5[t], neg_h_win[t][:, :S], ALU.add)
+            nc.scalar.activation(over[:], gap[:], ACT.Relu, scale=-1.0)
+            return over
+
+        def neg_lower(dst, t, g4, cols):
+            nc.vector.scalar_tensor_tensor(dst[:, cols], y_ps[t][:, cols], -1.0, g4[:, cols], ALU.mult, ALU.max)
+
+        overs = {t: excess_of_h(t) for t in (0, 1, LAST)}
+        whole = slice(0, S)
+        for t in range(2):
+            g4, lower, turned, res = (f32_tile(f"{name}{t}") for name in ("g4_", "lower", "turned", "res"))
+            nc.vector.tensor_copy(g4[:], neg_h_win[t][:].indirect(n4_sb[:]))
+            neg_lower(lower, t, g4, whole)
+            terms = [(term, c) for term in (g5[t], overs[t][:], lower[:]) for c in blocks]
+            for k, (term, c) in enumerate(terms):
+                nc.tensor.matmul(h_ps[t][:, c], lhsT=term[:, c], rhs=identity[:], is_transpose=True,
+                                 start=k == 0, stop=k == len(terms) - 1)
+            nc.scalar.copy(turned[:], h_ps[t][:])
+            for c in blocks:
+                nc.tensor.transpose(y_ps[t][:, c], turned[:, c], identity[:])
+            nc.scalar.copy(res[:], y_ps[t][:])
             nc.sync.dma_start(out_rows[:, t, :], res[:])
-            if t == 0:
-                nc.gpsimd.tensor_tensor(upper[LAST][:], h_win[LAST][:, :S], excess5[:], ALU.add)
+
+        upper_last = f32_tile("upper_last")
+        nc.gpsimd.tensor_tensor(upper_last[:], g5[LAST], overs[LAST][:], ALU.add)
+
+        g4, lower, upper = (f32_tile(f"{name}2") for name in ("g4_", "lower", "upper"))
+        nc.vector.tensor_copy(g4[:], neg_h_win[2][:].indirect(n4_sb[:]))
+        nc.vector.tensor_tensor(upper[:], h_ps[2][:], g5[2], ALU.max)
+        neg_lower(lower, 2, g4, whole)
+        res = overs[LAST]
+        nc.gpsimd.tensor_tensor(res[:], upper[:], lower[:], ALU.add)
+        nc.sync.dma_start(out_rows[:, 2, :], res[:])
+
         g4, lower, res = (f32_tile(f"{name}{LAST}") for name in ("g4_", "lower", "res"))
         for u, cols in enumerate(HALVES):
-            nc.vector.tensor_copy(g4[:, cols], h_win[LAST][:].indirect(n4_sb[:, 16 * u : 16 * (u + 1)]))
+            nc.vector.tensor_copy(g4[:, cols], neg_h_win[LAST][:].indirect(n4_sb[:, 16 * u : 16 * (u + 1)]))
         for cols in HALVES:
-            nc.vector.tensor_tensor(lower[:, cols], y_ps[LAST][:, cols], g4[:, cols], ALU.min)
+            neg_lower(lower, LAST, g4, cols)
         for cols in HALVES:
-            nc.vector.tensor_tensor(res[:, cols], upper[LAST][:, cols], lower[:, cols], ALU.subtract)
+            nc.vector.tensor_tensor(res[:, cols], upper_last[:, cols], lower[:, cols], ALU.add)
             nc.sync.dma_start(out_rows[:, LAST, cols], res[:, cols])

@@ -1,7 +1,6 @@
 from contextlib import ExitStack
 
 import concourse.mybir as mybir
-from concourse.masks import make_identity
 
 K, T, S, N, H = 512, 2048, 512, 512, 512
 FLOPS = 2 * K * H * S + 2 * H * N * S
@@ -45,15 +44,12 @@ def tile_picked_skipmaxbmix_none_p_kernel(tc, x_words, x_scales, w1, gn, w2, off
             nc.vector.quantize_mx(out=codes[:].bitcast(FP8X4), scales=scales[:], in_=values)
             return codes, scales
 
-        identity = keep.tile([P, P], F32, name="identity")
-        make_identity(nc, identity[:])
-
         xs_all = keep.tile([P, T], U8, name="xs_all")
         nc.vector.memset(xs_all[:].bitcast(I32), 0)
         w1_raw = keep.tile([P, PACK, H], F32, name="w1_raw")
         nc.sync.dma_start(w1_raw[:], w1.rearrange("(p j) c -> p j c", j=PACK))
-        for q in range(4):
-            nc.sync.dma_start(xs_all[32 * q : 32 * q + 4, :].bitcast(I32), x_scales[0, 4 * q : 4 * q + 4, :].bitcast(I32))
+        for r in range(4):
+            nc.sync.dma_start(xs_all[r:P:32, :].bitcast(I32), x_scales[0, r:16:4, :].bitcast(I32))
         offs_sb = load_list(offs, "offs_sb")
         xw_all = keep.tile([P, T], I32, name="xw_all", tag="xw_all", align_bytes=64)
         nc.sync.dma_start(xw_all[:], x_words[0].rearrange("p n t -> p (n t)").bitcast(I32))
@@ -162,54 +158,31 @@ def tile_picked_skipmaxbmix_none_p_kernel(tc, x_words, x_scales, w1, gn, w2, off
             for cols in HALVES if t == 0 else (slice(0, S),):
                 nc.tensor.matmul_mx(out=h_ps[t][:, cols], lhsT=w2_codes[:, rows].bitcast(FP8X4), lhsT_scale=w2_scales[:, rows],
                                     rhs=z_codes[:, cols].bitcast(FP8X4), rhs_scale=z_scales[:, cols], start=True, stop=True)
-        neg_h_win = [keep.tile([P, WINDOW], F32, name=f"neg_h_win{t}") for t in range(PACK)]
+        h_win = [keep.tile([P, WINDOW], F32, name=f"h_win{t}") for t in range(PACK)]
+        upper = [f32_tile(f"upper{t}") for t in range(PACK)]
         out_rows = out.rearrange("(p t) s -> p t s", t=PACK)
-        blocks = [slice(P * c, P * (c + 1)) for c in range(S // P)]
 
         for t in range(PACK):
-            nc.scalar.activation(neg_h_win[t][:, :S], h_ps[t][:], ACT.Copy, scale=-1.0)
-
-        def excess_of_h(t):
-            gap, over = f32_tile(f"gap{t}"), f32_tile(f"over{t}")
-            nc.gpsimd.tensor_tensor(gap[:], g5[t], neg_h_win[t][:, :S], ALU.add)
-            nc.scalar.activation(over[:], gap[:], ACT.Relu, scale=-1.0)
-            return over
-
-        def neg_lower(dst, t, g4, cols):
-            nc.vector.scalar_tensor_tensor(dst[:, cols], y_ps[t][:, cols], -1.0, g4[:, cols], ALU.mult, ALU.max)
-
-        overs = {t: excess_of_h(t) for t in (0, 1, LAST)}
-        whole = slice(0, S)
-        for t in range(2):
-            g4, lower, turned, res = (f32_tile(f"{name}{t}") for name in ("g4_", "lower", "turned", "res"))
-            nc.vector.tensor_copy(g4[:], neg_h_win[t][:].indirect(n4_sb[:]))
-            neg_lower(lower, t, g4, whole)
-            terms = [(term, c) for term in (g5[t], overs[t][:], lower[:]) for c in blocks]
-            for k, (term, c) in enumerate(terms):
-                nc.tensor.matmul(h_ps[t][:, c], lhsT=term[:, c], rhs=identity[:], is_transpose=True,
-                                 start=k == 0, stop=k == len(terms) - 1)
-            nc.scalar.copy(turned[:], h_ps[t][:])
-            for c in blocks:
-                nc.tensor.transpose(y_ps[t][:, c], turned[:, c], identity[:])
-            nc.scalar.copy(res[:], y_ps[t][:])
+            nc.scalar.copy(h_win[t][:, :S], h_ps[t][:])
+        diff5, excess5 = f32_tile("diff5"), f32_tile("excess5")
+        nc.gpsimd.tensor_tensor(diff5[:], g5[LAST], h_win[LAST][:, :S], ALU.subtract)
+        nc.scalar.activation(excess5[:], diff5[:], ACT.Relu)
+        res_tiles = (g5_last, excess5, f32_tile("res2"))
+        for t in range(LAST):
+            g4, lower = (f32_tile(f"{name}{t}") for name in ("g4_", "lower"))
+            res = res_tiles[t]
+            nc.vector.tensor_copy(g4[:], h_win[t][:].indirect(n4_sb[:]))
+            nc.vector.tensor_tensor(upper[t][:], h_ps[t][:], g5[t], ALU.max)
+            nc.vector.tensor_tensor(lower[:], y_ps[t][:], g4[:], ALU.min)
+            nc.gpsimd.tensor_tensor(res[:], upper[t][:], lower[:], ALU.subtract)
             nc.sync.dma_start(out_rows[:, t, :], res[:])
-
-        upper_last = f32_tile("upper_last")
-        nc.gpsimd.tensor_tensor(upper_last[:], g5[LAST], overs[LAST][:], ALU.add)
-
-        g4, lower, upper = (f32_tile(f"{name}2") for name in ("g4_", "lower", "upper"))
-        nc.vector.tensor_copy(g4[:], neg_h_win[2][:].indirect(n4_sb[:]))
-        nc.vector.tensor_tensor(upper[:], h_ps[2][:], g5[2], ALU.max)
-        neg_lower(lower, 2, g4, whole)
-        res = overs[LAST]
-        nc.gpsimd.tensor_tensor(res[:], upper[:], lower[:], ALU.add)
-        nc.sync.dma_start(out_rows[:, 2, :], res[:])
-
+            if t == 0:
+                nc.gpsimd.tensor_tensor(upper[LAST][:], h_win[LAST][:, :S], excess5[:], ALU.add)
         g4, lower, res = (f32_tile(f"{name}{LAST}") for name in ("g4_", "lower", "res"))
         for u, cols in enumerate(HALVES):
-            nc.vector.tensor_copy(g4[:, cols], neg_h_win[LAST][:].indirect(n4_sb[:, 16 * u : 16 * (u + 1)]))
+            nc.vector.tensor_copy(g4[:, cols], h_win[LAST][:].indirect(n4_sb[:, 16 * u : 16 * (u + 1)]))
         for cols in HALVES:
-            neg_lower(lower, LAST, g4, cols)
+            nc.vector.tensor_tensor(lower[:, cols], y_ps[LAST][:, cols], g4[:, cols], ALU.min)
         for cols in HALVES:
-            nc.vector.tensor_tensor(res[:, cols], upper_last[:, cols], lower[:, cols], ALU.add)
+            nc.vector.tensor_tensor(res[:, cols], upper[LAST][:, cols], lower[:, cols], ALU.subtract)
             nc.sync.dma_start(out_rows[:, LAST, cols], res[:, cols])

@@ -18,9 +18,13 @@ ACT = mybir.ActivationFunctionType
 P = 128
 PACK = 4
 LAST = PACK - 1
+GROUP = 16
+QUADRANT = 32
 WINDOW = 2 * S
 HALF = S // 2
 HALVES = (slice(0, HALF), slice(HALF, S))
+WHOLE = (slice(0, S),)
+W2_PIECES = 4
 
 
 def tile_picked_skipmaxbmix_none_p_kernel(tc, x_words, x_scales, w1, gn, w2, offs, n1, n2, n3, n4, n5, out):
@@ -33,26 +37,36 @@ def tile_picked_skipmaxbmix_none_p_kernel(tc, x_words, x_scales, w1, gn, w2, off
             return keep.tile([P, S], F32, name=name)
 
         def load_list(src, name):
-            tile = keep.tile([P, S // 16], U16, name=name)
+            tile = keep.tile([P, S // GROUP], U16, name=name)
             nc.sync.dma_start(tile[:], src)
             return tile
 
-        def quantize(values, name, tag=None):
+        def gather(dst, window, offsets, cols=slice(0, S)):
+            entries = offsets[:, cols.start // GROUP : cols.stop // GROUP]
+            nc.vector.tensor_copy(dst[:, cols], window.indirect(entries))
+
+        def quantize(values, name, slot):
             width = values.shape[1] // PACK
-            codes = keep.tile([P, width], U32, name=f"{name}_codes", tag=tag or f"{name}_codes", align_bytes=64)
+            codes = keep.tile([P, width], U32, name=f"{name}_codes", tag=slot, align_bytes=64)
             scales = keep.tile([P, width], U8, name=f"{name}_scales", align_bytes=64)
             nc.vector.quantize_mx(out=codes[:].bitcast(FP8X4), scales=scales[:], in_=values)
             return codes, scales
 
-        xs_all = keep.tile([P, T], U8, name="xs_all")
-        nc.vector.memset(xs_all[:].bitcast(I32), 0)
+        def product(dst, weights, place, codes, scales):
+            w_codes, w_scales = weights
+            w_cols = slice(P * place, P * (place + 1))
+            nc.tensor.matmul_mx(out=dst, lhsT=w_codes[:, w_cols].bitcast(FP8X4), lhsT_scale=w_scales[:, w_cols],
+                                rhs=codes.bitcast(FP8X4), rhs_scale=scales, start=True, stop=True)
+
+        x_scales_all = keep.tile([P, T], U8, name="x_scales_all")
+        nc.vector.memset(x_scales_all[:].bitcast(I32), 0)
         w1_raw = keep.tile([P, PACK, H], F32, name="w1_raw")
         nc.sync.dma_start(w1_raw[:], w1.rearrange("(p j) c -> p j c", j=PACK))
-        for r in range(4):
-            nc.sync.dma_start(xs_all[r:P:32, :].bitcast(I32), x_scales[0, r:16:4, :].bitcast(I32))
+        for r in range(PACK):
+            nc.sync.dma_start(x_scales_all[r:P:QUADRANT, :].bitcast(I32), x_scales[0, r : K // 32 : PACK, :].bitcast(I32))
         offs_sb = load_list(offs, "offs_sb")
-        xw_all = keep.tile([P, T], I32, name="xw_all", tag="xw_all", align_bytes=64)
-        nc.sync.dma_start(xw_all[:], x_words[0].rearrange("p n t -> p (n t)").bitcast(I32))
+        x_words_all = keep.tile([P, T], I32, name="x_words_all", tag="x_words_all", align_bytes=64)
+        nc.sync.dma_start(x_words_all[:], x_words[0].rearrange("p n t -> p (n t)").bitcast(I32))
         n2_sb = load_list(n2, "n2_sb")
         n3_sb = load_list(n3, "n3_sb")
         n1_sb = load_list(n1, "n1_sb")
@@ -64,23 +78,20 @@ def tile_picked_skipmaxbmix_none_p_kernel(tc, x_words, x_scales, w1, gn, w2, off
         n4_sb = load_list(n4, "n4_sb")
 
         w1_view = w1_raw[:].rearrange("p j (m t) -> p m j t", t=PACK)
-        w1_bf = [keep.tile([P, 2 * PACK * P], BF16, name=f"w1_bf{u}", align_bytes=64) for u in range(2)]
-        w1_out = [tile[:].rearrange("p (t m j) -> p m j t", t=2, j=PACK) for tile in w1_bf]
-        nc.vector.tensor_copy(w1_out[0], w1_view[:, :, :, 0:2])
-        nc.scalar.copy(w1_out[1], w1_view[:, :, :, 2:4])
-        xs = keep.tile([P, S], U8, name="xs", align_bytes=64)
-        nc.vector.tensor_copy(xs[:], xs_all[:].indirect(offs_sb[:]))
-        w1_q = [quantize(w1_bf[0][:], "w1a")]
-        xw = keep.tile([P, S], U32, name="xw", tag="xw_then_w2", align_bytes=64)
-        for u, cols in enumerate(HALVES):
-            nc.vector.tensor_copy(xw[:, cols], xw_all[:].bitcast(U32).indirect(offs_sb[:, 16 * u : 16 * (u + 1)]))
-        w1_q.append(quantize(w1_bf[1][:], "w1b", tag="xw_all"))
+        w1_bf = [keep.tile([P, 2 * PACK * P], BF16, name=f"w1_bf{pair}", align_bytes=64) for pair in range(2)]
+        w1_dealt = [tile[:].rearrange("p (t m j) -> p m j t", t=2, j=PACK) for tile in w1_bf]
+        nc.vector.tensor_copy(w1_dealt[0], w1_view[:, :, :, 0:2])
+        nc.scalar.copy(w1_dealt[1], w1_view[:, :, :, 2:4])
+        x_scales_picked = keep.tile([P, S], U8, name="x_scales_picked", align_bytes=64)
+        gather(x_scales_picked, x_scales_all[:], offs_sb)
+        w1_mx = [quantize(w1_bf[0][:], "w1_pair0", "w1_pair0_codes")]
+        x_words_picked = keep.tile([P, S], U32, name="x_words_picked", tag="x_words_picked", align_bytes=64)
+        for cols in HALVES:
+            gather(x_words_picked, x_words_all[:].bitcast(U32), offs_sb, cols)
+        w1_mx.append(quantize(w1_bf[1][:], "w1_pair1", "x_words_all"))
 
         def y_product(bank, t, cols):
-            codes, scales = w1_q[t // 2]
-            rows = slice(P * (t % 2), P * (t % 2 + 1))
-            nc.tensor.matmul_mx(out=bank[:, cols], lhsT=codes[:, rows].bitcast(FP8X4), lhsT_scale=scales[:, rows],
-                                rhs=xw[:, cols].bitcast(FP8X4), rhs_scale=xs[:, cols], start=True, stop=True)
+            product(bank[:, cols], w1_mx[t // 2], t % 2, x_words_picked[:, cols], x_scales_picked[:, cols])
 
         y_ps = [psum.tile([P, S], F32, name=f"y_ps{t}") for t in range(PACK)]
         h_ps = [psum.tile([P, S], F32, name=f"h_ps{t}") for t in range(PACK)]
@@ -94,95 +105,107 @@ def tile_picked_skipmaxbmix_none_p_kernel(tc, x_words, x_scales, w1, gn, w2, off
         y_product(y_ps[0], 0, HALVES[0])
 
         z_bf = [keep.tile([P, HALF, PACK], BF16, name="z_bf0", align_bytes=64),
-                keep.tile([P, HALF, PACK], BF16, name="z_bf1", tag="z_then_g5", align_bytes=64)]
-        g2_tiles, excess_tiles, max23_tiles, g1_tiles = [], [], [], []
+                keep.tile([P, HALF, PACK], BF16, name="z_bf1", tag="z_bf1", align_bytes=64)]
+        y_n1, y_n2, excess23, max23, max01 = [], [], [], [], []
 
         def start_max23(t):
-            g2, g3, excess = (f32_tile(f"{name}{t}") for name in ("g2_", "g3_", "excess"))
-            diff = excess_tiles[t - 1] if t else f32_tile("diff0")
-            nc.vector.tensor_copy(g2[:], y_win[t][:].indirect(n2_sb[:]))
-            nc.vector.tensor_copy(g3[:], y_win[t][:].indirect(n3_sb[:]))
-            for cols in HALVES if t == 0 else (slice(0, S),):
-                nc.gpsimd.tensor_tensor(diff[:, cols], g3[:, cols], g2[:, cols], ALU.subtract)
+            at_n2, at_n3, excess = (f32_tile(f"{name}{t}") for name in ("y_n2_", "y_n3_", "excess23_"))
+            diff = excess23[t - 1] if t else f32_tile("diff23_0")
+            for cols in HALVES if t == 0 else WHOLE:
+                gather(at_n2, y_win[t][:], n2_sb, cols)
+                gather(at_n3, y_win[t][:], n3_sb, cols)
+                nc.gpsimd.tensor_tensor(diff[:, cols], at_n3[:, cols], at_n2[:, cols], ALU.subtract)
                 nc.scalar.activation(excess[:, cols], diff[:, cols], ACT.Relu)
-            g2_tiles.append(g2)
-            excess_tiles.append(excess)
+            y_n2.append(at_n2)
+            excess23.append(excess)
 
         def finish_max23(t):
             larger = f32_tile(f"max23_{t}")
-            for cols in HALVES if t == 0 else (slice(0, S),):
-                nc.gpsimd.tensor_tensor(larger[:, cols], g2_tiles[t][:, cols], excess_tiles[t][:, cols], ALU.add)
-            max23_tiles.append(larger)
+            for cols in HALVES if t == 0 else WHOLE:
+                nc.gpsimd.tensor_tensor(larger[:, cols], y_n2[t][:, cols], excess23[t][:, cols], ALU.add)
+            max23.append(larger)
+
+        def gather_n1(t):
+            at_n1 = f32_tile(f"y_n1_{t}")
+            gather(at_n1, y_win[t][:], n1_sb)
+            y_n1.append(at_n1)
 
         def z_tile(t):
-            g1, max01, zraw = (f32_tile(f"{name}{t}") for name in ("g1_", "max01_", "zraw"))
-            g1_tiles.append(g1)
-            nc.vector.tensor_copy(g1[:], y_win[t][:].indirect(n1_sb[:]))
-            nc.vector.tensor_tensor(max01[:], y_ps[t][:], g1[:], ALU.max)
-            for cols in HALVES if t == LAST else (slice(0, S),):
-                nc.gpsimd.tensor_tensor(zraw[:, cols], max01[:, cols], max23_tiles[t][:, cols], ALU.subtract)
-            for u, cols in enumerate(HALVES):
-                nc.scalar.activation(z_bf[u][:, :, t], zraw[:, cols], ACT.Copy, scale=gn_sb[:, t : t + 1])
+            larger = f32_tile(f"max01_{t}")
+            unscaled = max01[t - 1] if t == LAST else f32_tile(f"unscaled{t}")
+            max01.append(larger)
+            nc.vector.tensor_tensor(larger[:], y_ps[t][:], y_n1[t][:], ALU.max)
+            for cols in HALVES if t == LAST else WHOLE:
+                nc.gpsimd.tensor_tensor(unscaled[:, cols], larger[:, cols], max23[t][:, cols], ALU.subtract)
+            for half, cols in enumerate(HALVES):
+                nc.scalar.activation(z_bf[half][:, :, t], unscaled[:, cols], ACT.Copy, scale=gn_sb[:, t : t + 1])
 
         start_max23(0)
         finish_max23(0)
-        for t in range(PACK):
-            if t < LAST:
-                start_max23(t + 1)
+        for t in range(LAST - 1):
+            start_max23(t + 1)
+            gather_n1(t)
             z_tile(t)
-            if t < LAST:
-                finish_max23(t + 1)
+            finish_max23(t + 1)
+        y_n2_last, y_n3_last, max23_last = (f32_tile(name) for name in ("y_n2_last", "y_n3_last", "max23_last"))
+        gather_n1(LAST - 1)
+        gather(y_n2_last, y_win[LAST][:], n2_sb)
+        z_tile(LAST - 1)
+        gather(y_n3_last, y_win[LAST][:], n3_sb)
+        gather_n1(LAST)
+        nc.vector.tensor_tensor(max23_last[:], y_n2_last[:], y_n3_last[:], ALU.max)
+        max23.append(max23_last)
+        z_tile(LAST)
 
-        w2_bf = keep.tile([P, PACK * N], BF16, name="w2_bf", tag="xw_then_w2", align_bytes=64)
-        for piece in range(4):
-            ms = slice(32 * piece, 32 * (piece + 1))
+        w2_bf = keep.tile([P, PACK * N], BF16, name="w2_bf", tag="x_words_picked", align_bytes=64)
+        for piece in range(W2_PIECES):
+            ms = slice(P // W2_PIECES * piece, P // W2_PIECES * (piece + 1))
             nc.scalar.copy(
                 w2_bf[:].rearrange("p (t m j) -> p m j t", t=PACK, j=PACK)[:, ms],
                 w2_raw[:].rearrange("p j (m t) -> p m j t", t=PACK)[:, ms],
             )
-        g5 = [g1_tiles[LAST - 1][:], g1_tiles[LAST][:], y_win[0][:, S:]]
+
+        y_n5 = [y_n3_last[:], y_n1[LAST][:], y_win[0][:, S:]]
         for t in range(LAST):
-            nc.vector.tensor_copy(g5[t], y_win[t][:].indirect(n5_sb[:]))
-        w2_codes, w2_scales = quantize(w2_bf[:], "w2", tag="y_win1")
+            gather(y_n5[t], y_win[t][:], n5_sb)
+        w2_mx = quantize(w2_bf[:], "w2", "y_win1")
         z_codes = keep.tile([P, S], U32, name="z_codes", align_bytes=64)
         z_scales = keep.tile([P, S], U8, name="z_scales", align_bytes=64)
-        for u, half in enumerate(HALVES):
-            nc.vector.quantize_mx(out=z_codes[:, half].bitcast(FP8X4), scales=z_scales[:, half],
-                                  in_=z_bf[u][:].rearrange("p s t -> p (s t)"))
-        g5_last = keep.tile([P, S], F32, name="g5_last", tag="z_then_g5", align_bytes=64)
-        g5.append(g5_last[:])
-        nc.vector.tensor_copy(g5[LAST], y_win[LAST][:].indirect(n5_sb[:]))
+        for half, cols in enumerate(HALVES):
+            nc.vector.quantize_mx(out=z_codes[:, cols].bitcast(FP8X4), scales=z_scales[:, cols],
+                                  in_=z_bf[half][:].rearrange("p s t -> p (s t)"))
+        y_n5_last = keep.tile([P, S], F32, name="y_n5_last", tag="z_bf1", align_bytes=64)
+        y_n5.append(y_n5_last[:])
+        gather(y_n5_last, y_win[LAST][:], n5_sb)
 
-        for t in range(PACK):
-            rows = slice(P * t, P * (t + 1))
-            for cols in HALVES if t == 0 else (slice(0, S),):
-                nc.tensor.matmul_mx(out=h_ps[t][:, cols], lhsT=w2_codes[:, rows].bitcast(FP8X4), lhsT_scale=w2_scales[:, rows],
-                                    rhs=z_codes[:, cols].bitcast(FP8X4), rhs_scale=z_scales[:, cols], start=True, stop=True)
+        h_order = (0, LAST, *range(1, LAST))
+        for t in h_order:
+            for cols in HALVES if t == 0 else WHOLE:
+                product(h_ps[t][:, cols], w2_mx, t, z_codes[:, cols], z_scales[:, cols])
         h_win = [keep.tile([P, WINDOW], F32, name=f"h_win{t}") for t in range(PACK)]
         upper = [f32_tile(f"upper{t}") for t in range(PACK)]
         out_rows = out.rearrange("(p t) s -> p t s", t=PACK)
-
-        for t in range(PACK):
+        for t in h_order:
             nc.scalar.copy(h_win[t][:, :S], h_ps[t][:])
+
         diff5, excess5 = f32_tile("diff5"), f32_tile("excess5")
-        nc.gpsimd.tensor_tensor(diff5[:], g5[LAST], h_win[LAST][:, :S], ALU.subtract)
+        nc.gpsimd.tensor_tensor(diff5[:], y_n5[LAST], h_win[LAST][:, :S], ALU.subtract)
         nc.scalar.activation(excess5[:], diff5[:], ACT.Relu)
-        res_tiles = (g5_last, excess5, f32_tile("res2"))
+        results = (y_n5_last, excess5, f32_tile("result2"))
         for t in range(LAST):
-            g4, lower = (f32_tile(f"{name}{t}") for name in ("g4_", "lower"))
-            res = res_tiles[t]
-            nc.vector.tensor_copy(g4[:], h_win[t][:].indirect(n4_sb[:]))
-            nc.vector.tensor_tensor(upper[t][:], h_ps[t][:], g5[t], ALU.max)
-            nc.vector.tensor_tensor(lower[:], y_ps[t][:], g4[:], ALU.min)
-            nc.gpsimd.tensor_tensor(res[:], upper[t][:], lower[:], ALU.subtract)
-            nc.sync.dma_start(out_rows[:, t, :], res[:])
+            h_n4, lower = (f32_tile(f"{name}{t}") for name in ("h_n4_", "lower"))
+            gather(h_n4, h_win[t][:], n4_sb)
+            nc.vector.tensor_tensor(upper[t][:], h_ps[t][:], y_n5[t], ALU.max)
+            nc.vector.tensor_tensor(lower[:], y_ps[t][:], h_n4[:], ALU.min)
+            nc.gpsimd.tensor_tensor(results[t][:], upper[t][:], lower[:], ALU.subtract)
+            nc.sync.dma_start(out_rows[:, t, :], results[t][:])
             if t == 0:
                 nc.gpsimd.tensor_tensor(upper[LAST][:], h_win[LAST][:, :S], excess5[:], ALU.add)
-        g4, lower, res = (f32_tile(f"{name}{LAST}") for name in ("g4_", "lower", "res"))
-        for u, cols in enumerate(HALVES):
-            nc.vector.tensor_copy(g4[:, cols], h_win[LAST][:].indirect(n4_sb[:, 16 * u : 16 * (u + 1)]))
+        h_n4, lower, result = (f32_tile(f"{name}{LAST}") for name in ("h_n4_", "lower", "result"))
         for cols in HALVES:
-            nc.vector.tensor_tensor(lower[:, cols], y_ps[LAST][:, cols], g4[:, cols], ALU.min)
+            gather(h_n4, h_win[LAST][:], n4_sb, cols)
         for cols in HALVES:
-            nc.vector.tensor_tensor(res[:, cols], upper[LAST][:, cols], lower[:, cols], ALU.subtract)
-            nc.sync.dma_start(out_rows[:, LAST, cols], res[:, cols])
+            nc.vector.tensor_tensor(lower[:, cols], y_ps[LAST][:, cols], h_n4[:, cols], ALU.min)
+        for cols in HALVES:
+            nc.vector.tensor_tensor(result[:, cols], upper[LAST][:, cols], lower[:, cols], ALU.subtract)
+            nc.sync.dma_start(out_rows[:, LAST, cols], result[:, cols])

from contextlib import ExitStack

import concourse.mybir as mybir

K, T, S, N, H = 512, 2048, 512, 512, 512
FLOPS = 2 * K * H * S + 2 * H * N * S

F32 = mybir.dt.float32
BF16 = mybir.dt.bfloat16
I32 = mybir.dt.int32
U32 = mybir.dt.uint32
U16 = mybir.dt.uint16
U8 = mybir.dt.uint8
FP8X4 = mybir.dt.float8_e4m3fn_x4
ALU = mybir.AluOpType
ACT = mybir.ActivationFunctionType

P = 128
PACK = 4
LAST = PACK - 1
GROUP = 16
QUADRANT = 32
WINDOW = 2 * S
HALF = S // 2
HALVES = (slice(0, HALF), slice(HALF, S))
WHOLE = (slice(0, S),)
W2_PIECES = 4


def tile_picked_skipmaxbmix_none_p_kernel(tc, x_words, x_scales, w1, gn, w2, offs, n1, n2, n3, n4, n5, out):
    nc = tc.nc
    with ExitStack() as ctx:
        keep = ctx.enter_context(tc.tile_pool(name="keep", bufs=1))
        psum = ctx.enter_context(tc.psum_pool(name="psum", bufs=1))

        def f32_tile(name):
            return keep.tile([P, S], F32, name=name)

        def load_list(src, name):
            tile = keep.tile([P, S // GROUP], U16, name=name)
            nc.sync.dma_start(tile[:], src)
            return tile

        def gather(dst, window, offsets, cols=slice(0, S)):
            entries = offsets[:, cols.start // GROUP : cols.stop // GROUP]
            nc.vector.tensor_copy(dst[:, cols], window.indirect(entries))

        def quantize(values, name, slot):
            width = values.shape[1] // PACK
            codes = keep.tile([P, width], U32, name=f"{name}_codes", tag=slot, align_bytes=64)
            scales = keep.tile([P, width], U8, name=f"{name}_scales", align_bytes=64)
            nc.vector.quantize_mx(out=codes[:].bitcast(FP8X4), scales=scales[:], in_=values)
            return codes, scales

        def product(dst, weights, place, codes, scales):
            w_codes, w_scales = weights
            w_cols = slice(P * place, P * (place + 1))
            nc.tensor.matmul_mx(out=dst, lhsT=w_codes[:, w_cols].bitcast(FP8X4), lhsT_scale=w_scales[:, w_cols],
                                rhs=codes.bitcast(FP8X4), rhs_scale=scales, start=True, stop=True)

        x_scales_all = keep.tile([P, T], U8, name="x_scales_all")
        nc.vector.memset(x_scales_all[:].bitcast(I32), 0)
        w1_raw = keep.tile([P, PACK, H], F32, name="w1_raw")
        nc.sync.dma_start(w1_raw[:], w1.rearrange("(p j) c -> p j c", j=PACK))
        for r in range(PACK):
            nc.sync.dma_start(x_scales_all[r:P:QUADRANT, :].bitcast(I32), x_scales[0, r : K // 32 : PACK, :].bitcast(I32))
        offs_sb = load_list(offs, "offs_sb")
        x_words_all = keep.tile([P, T], I32, name="x_words_all", tag="x_words_all", align_bytes=64)
        nc.sync.dma_start(x_words_all[:], x_words[0].rearrange("p n t -> p (n t)").bitcast(I32))
        n2_sb = load_list(n2, "n2_sb")
        n3_sb = load_list(n3, "n3_sb")
        n1_sb = load_list(n1, "n1_sb")
        w2_raw = keep.tile([P, PACK, N], F32, name="w2_raw")
        nc.sync.dma_start(w2_raw[:], w2.rearrange("(p j) c -> p j c", j=PACK))
        gn_sb = keep.tile([P, PACK], F32, name="gn_sb")
        nc.sync.dma_start(gn_sb[:], gn.rearrange("(p t) o -> p (t o)", t=PACK))
        n5_sb = load_list(n5, "n5_sb")
        n4_sb = load_list(n4, "n4_sb")

        w1_view = w1_raw[:].rearrange("p j (m t) -> p m j t", t=PACK)
        w1_bf = [keep.tile([P, 2 * PACK * P], BF16, name=f"w1_bf{pair}", align_bytes=64) for pair in range(2)]
        w1_dealt = [tile[:].rearrange("p (t m j) -> p m j t", t=2, j=PACK) for tile in w1_bf]
        nc.vector.tensor_copy(w1_dealt[0], w1_view[:, :, :, 0:2])
        nc.scalar.copy(w1_dealt[1], w1_view[:, :, :, 2:4])
        x_scales_picked = keep.tile([P, S], U8, name="x_scales_picked", align_bytes=64)
        gather(x_scales_picked, x_scales_all[:], offs_sb)
        w1_mx = [quantize(w1_bf[0][:], "w1_pair0", "w1_pair0_codes")]
        x_words_picked = keep.tile([P, S], U32, name="x_words_picked", tag="x_words_picked", align_bytes=64)
        for cols in HALVES:
            gather(x_words_picked, x_words_all[:].bitcast(U32), offs_sb, cols)
        w1_mx.append(quantize(w1_bf[1][:], "w1_pair1", "x_words_all"))

        def y_product(bank, t, cols):
            product(bank[:, cols], w1_mx[t // 2], t % 2, x_words_picked[:, cols], x_scales_picked[:, cols])

        y_ps = [psum.tile([P, S], F32, name=f"y_ps{t}") for t in range(PACK)]
        h_ps = [psum.tile([P, S], F32, name=f"h_ps{t}") for t in range(PACK)]
        y_win = [keep.tile([P, WINDOW], F32, name=f"y_win{t}", tag=f"y_win{t}", align_bytes=64) for t in range(PACK)]
        for bank, cols in zip((h_ps[LAST], y_ps[0]), HALVES):
            y_product(bank, 0, cols)
            nc.scalar.copy(y_win[0][:, cols], bank[:, cols])
        for t in range(1, PACK):
            y_product(y_ps[t], t, slice(0, S))
            nc.scalar.copy(y_win[t][:, :S], y_ps[t][:])
        y_product(y_ps[0], 0, HALVES[0])

        z_bf = [keep.tile([P, HALF, PACK], BF16, name="z_bf0", align_bytes=64),
                keep.tile([P, HALF, PACK], BF16, name="z_bf1", tag="z_bf1", align_bytes=64)]
        y_n1, y_n2, excess23, max23, max01 = [], [], [], [], []

        def start_max23(t):
            at_n2, at_n3, excess = (f32_tile(f"{name}{t}") for name in ("y_n2_", "y_n3_", "excess23_"))
            diff = excess23[t - 1] if t else f32_tile("diff23_0")
            for cols in HALVES if t == 0 else WHOLE:
                gather(at_n2, y_win[t][:], n2_sb, cols)
                gather(at_n3, y_win[t][:], n3_sb, cols)
                nc.gpsimd.tensor_tensor(diff[:, cols], at_n3[:, cols], at_n2[:, cols], ALU.subtract)
                nc.scalar.activation(excess[:, cols], diff[:, cols], ACT.Relu)
            y_n2.append(at_n2)
            excess23.append(excess)

        def finish_max23(t):
            larger = f32_tile(f"max23_{t}")
            for cols in HALVES if t == 0 else WHOLE:
                nc.gpsimd.tensor_tensor(larger[:, cols], y_n2[t][:, cols], excess23[t][:, cols], ALU.add)
            max23.append(larger)

        def gather_n1(t):
            at_n1 = f32_tile(f"y_n1_{t}")
            gather(at_n1, y_win[t][:], n1_sb)
            y_n1.append(at_n1)

        def z_tile(t):
            larger = f32_tile(f"max01_{t}")
            unscaled = max01[t - 1] if t == LAST else f32_tile(f"unscaled{t}")
            max01.append(larger)
            nc.vector.tensor_tensor(larger[:], y_ps[t][:], y_n1[t][:], ALU.max)
            for cols in HALVES if t == LAST else WHOLE:
                nc.gpsimd.tensor_tensor(unscaled[:, cols], larger[:, cols], max23[t][:, cols], ALU.subtract)
            for half, cols in enumerate(HALVES):
                nc.scalar.activation(z_bf[half][:, :, t], unscaled[:, cols], ACT.Copy, scale=gn_sb[:, t : t + 1])

        start_max23(0)
        finish_max23(0)
        for t in range(LAST - 1):
            start_max23(t + 1)
            gather_n1(t)
            z_tile(t)
            finish_max23(t + 1)
        y_n2_last, y_n3_last, max23_last = (f32_tile(name) for name in ("y_n2_last", "y_n3_last", "max23_last"))
        gather_n1(LAST - 1)
        gather(y_n2_last, y_win[LAST][:], n2_sb)
        z_tile(LAST - 1)
        gather(y_n3_last, y_win[LAST][:], n3_sb)
        gather_n1(LAST)
        nc.vector.tensor_tensor(max23_last[:], y_n2_last[:], y_n3_last[:], ALU.max)
        max23.append(max23_last)
        z_tile(LAST)

        w2_bf = keep.tile([P, PACK * N], BF16, name="w2_bf", tag="x_words_picked", align_bytes=64)
        for piece in range(W2_PIECES):
            ms = slice(P // W2_PIECES * piece, P // W2_PIECES * (piece + 1))
            nc.scalar.copy(
                w2_bf[:].rearrange("p (t m j) -> p m j t", t=PACK, j=PACK)[:, ms],
                w2_raw[:].rearrange("p j (m t) -> p m j t", t=PACK)[:, ms],
            )

        y_n5 = [y_n3_last[:], y_n1[LAST][:], y_win[0][:, S:]]
        for t in range(LAST):
            gather(y_n5[t], y_win[t][:], n5_sb)
        w2_mx = quantize(w2_bf[:], "w2", "y_win1")
        z_codes = keep.tile([P, S], U32, name="z_codes", align_bytes=64)
        z_scales = keep.tile([P, S], U8, name="z_scales", align_bytes=64)
        for half, cols in enumerate(HALVES):
            nc.vector.quantize_mx(out=z_codes[:, cols].bitcast(FP8X4), scales=z_scales[:, cols],
                                  in_=z_bf[half][:].rearrange("p s t -> p (s t)"))
        y_n5_last = keep.tile([P, S], F32, name="y_n5_last", tag="z_bf1", align_bytes=64)
        y_n5.append(y_n5_last[:])
        gather(y_n5_last, y_win[LAST][:], n5_sb)

        h_order = (0, LAST, *range(1, LAST))
        for t in h_order:
            for cols in HALVES if t == 0 else WHOLE:
                product(h_ps[t][:, cols], w2_mx, t, z_codes[:, cols], z_scales[:, cols])
        h_win = [keep.tile([P, WINDOW], F32, name=f"h_win{t}") for t in range(PACK)]
        upper = [f32_tile(f"upper{t}") for t in range(PACK)]
        out_rows = out.rearrange("(p t) s -> p t s", t=PACK)
        for t in h_order:
            nc.scalar.copy(h_win[t][:, :S], h_ps[t][:])

        diff5, excess5 = f32_tile("diff5"), f32_tile("excess5")
        nc.gpsimd.tensor_tensor(diff5[:], y_n5[LAST], h_win[LAST][:, :S], ALU.subtract)
        nc.scalar.activation(excess5[:], diff5[:], ACT.Relu)
        results = (y_n5_last, excess5, f32_tile("result2"))
        for t in range(LAST):
            h_n4, lower = (f32_tile(f"{name}{t}") for name in ("h_n4_", "lower"))
            gather(h_n4, h_win[t][:], n4_sb)
            nc.vector.tensor_tensor(upper[t][:], h_ps[t][:], y_n5[t], ALU.max)
            nc.vector.tensor_tensor(lower[:], y_ps[t][:], h_n4[:], ALU.min)
            nc.gpsimd.tensor_tensor(results[t][:], upper[t][:], lower[:], ALU.subtract)
            nc.sync.dma_start(out_rows[:, t, :], results[t][:])
            if t == 0:
                nc.gpsimd.tensor_tensor(upper[LAST][:], h_win[LAST][:, :S], excess5[:], ALU.add)
        h_n4, lower, result = (f32_tile(f"{name}{LAST}") for name in ("h_n4_", "lower", "result"))
        for cols in HALVES:
            gather(h_n4, h_win[LAST][:], n4_sb, cols)
        for cols in HALVES:
            nc.vector.tensor_tensor(lower[:, cols], y_ps[LAST][:, cols], h_n4[:, cols], ALU.min)
        for cols in HALVES:
            nc.vector.tensor_tensor(result[:, cols], upper[LAST][:, cols], lower[:, cols], ALU.subtract)
            nc.sync.dma_start(out_rows[:, LAST, cols], result[:, cols])
